import numpy as np
import ml_dtypes

BF16 = ml_dtypes.bfloat16


def bf(x):
    return np.asarray(x, np.float32).astype(BF16)


def f32(x):
    return np.asarray(x, np.float32)


def f64(x):
    return np.asarray(x).astype(np.float64)


def striped(idx):
    return np.tile(idx.reshape(-1, 16).T, (8, 1))


S, K, M, N, D, V = 1024, 256, 512, 1024, 16, 64


def gelu_tanh(v):
    return 0.5 * v * (1.0 + np.tanh(np.sqrt(2.0 / np.pi) * (v + 0.044715 * v**3)))


def setup_inputs():
    return {"table": bf(np.random.standard_normal((K, S))), "w": bf(np.random.standard_normal((K, M)) / np.sqrt(K)), "b": f32(0.5 * np.random.standard_normal((M, 1))), "offs": striped(np.random.permutation(np.tile(np.arange(S), 2))[:N])}


def reference(table, w, b, offs):
    idx = offs[:16].T.reshape(-1)
    x = f64(table)[:, idx]
    y = f64(w).T @ x
    z = gelu_tanh(y + f64(b))
    return z.reshape(M, V, D).max(axis=2)

@@ -1,0 +1,78 @@
+import concourse.mybir as mybir
+
+BF16, F32, U16 = mybir.dt.bfloat16, mybir.dt.float32, mybir.dt.uint16
+GELU = mybir.ActivationFunctionType.Gelu_apprx_tanh
+
+P = 128
+K, S = 256, 1024
+M, N = 512, 1024
+NEIGHBOURS = 16
+PIECE = 512
+K_BLOCKS, M_BLOCKS, PIECES = K // P, M // P, N // PIECE
+OFFSET_COLUMNS = PIECE // 16
+STEP = PIECE // 8
+
+FLOPS = 2 * K * M * N
+
+
+def tile_gather_matmul_kernel(tc, table, w, b, offs, out):
+    nc = tc.nc
+    with (
+        tc.tile_pool(name="held", bufs=1) as held,
+        tc.tile_pool(name="work", bufs=8) as work,
+        tc.psum_pool(name="psum", bufs=4) as psum,
+    ):
+        offsets = held.tile([P, N // 16], U16, name="offsets")
+        windows = [held.tile([P, S], BF16, name=f"window{kb}") for kb in range(K_BLOCKS)]
+        weights_first = held.tile([P, K_BLOCKS, P], BF16, name="weights_first")
+        weights_rest = held.tile([P, K_BLOCKS, M - P], BF16, name="weights_rest")
+        w_by_block = w.rearrange("(kb p) m -> p kb m", p=P)
+        bias = held.tile([P, M_BLOCKS], F32, name="bias")
+        nc.sync.dma_start(windows[0][:], table[0:P, :])
+        nc.scalar.dma_start(weights_first[:], w_by_block[:, :, 0:P])
+        nc.sync.dma_start(offsets[:], offs)
+        nc.sync.dma_start(windows[1][:], table[P : 2 * P, :])
+        nc.scalar.dma_start(weights_rest[:], w_by_block[:, :, P:M])
+        nc.sync.dma_start(bias[:], b.rearrange("(mb p) o -> p (mb o)", p=P))
+
+        def weights(kb, mb):
+            if mb == 0:
+                return weights_first[:, kb, :]
+            return weights_rest[:, kb, (mb - 1) * P : mb * P]
+
+        picked = [
+            offsets[:, piece * OFFSET_COLUMNS : (piece + 1) * OFFSET_COLUMNS] for piece in range(PIECES)
+        ]
+        for mb in range(M_BLOCKS):
+            banks = [psum.tile([P, PIECE], F32, name=f"bank{piece}") for piece in range(PIECES)]
+            if mb == 0:
+                order = [(kb, piece) for kb in range(K_BLOCKS) for piece in range(PIECES)]
+            else:
+                order = [(kb, piece) for piece in range(PIECES) for kb in range(K_BLOCKS)]
+            for kb, piece in order:
+                nc.tensor.matmul(
+                    banks[piece][:],
+                    weights(kb, mb),
+                    windows[kb][:].indirect(picked[piece]),
+                    start=(kb == 0),
+                    stop=(kb == K_BLOCKS - 1),
+                )
+            for piece in range(PIECES):
+                pooled = work.tile([P, PIECE // NEIGHBOURS], F32, name="pooled")
+                for step in range(PIECE // STEP):
+                    z = work.tile([P, STEP], F32, name="z")
+                    nc.scalar.activation(
+                        z[:],
+                        banks[piece][:, step * STEP : (step + 1) * STEP],
+                        GELU,
+                        bias=bias[:, mb : mb + 1],
+                    )
+                    first = step * STEP // NEIGHBOURS
+                    nc.vector.tensor_reduce(
+                        pooled[:, first : first + STEP // NEIGHBOURS],
+                        z[:].rearrange("p (v t) -> p v t", t=NEIGHBOURS),
+                        axis=mybir.AxisListType.X,
+                        op=mybir.AluOpType.max,
+                    )
+                nodes = PIECE // NEIGHBOURS
+                nc.sync.dma_start(out[mb * P : (mb + 1) * P, piece * nodes : (piece + 1) * nodes], pooled[:])

@@ -24,12 +24,13 @@ def tile_gather_matmul_kernel(tc, table, w, b, offs, out):
     ):
         offsets = held.tile([P, N // 16], U16, name="offsets")
         windows = [held.tile([P, S], BF16, name=f"window{kb}") for kb in range(K_BLOCKS)]
-        weights_first = held.tile([P, K_BLOCKS, P], BF16, name="weights_first")
+        weights_first = [held.tile([P, P], BF16, name=f"weights_first{kb}") for kb in range(K_BLOCKS)]
         weights_rest = held.tile([P, K_BLOCKS, M - P], BF16, name="weights_rest")
         w_by_block = w.rearrange("(kb p) m -> p kb m", p=P)
         bias = held.tile([P, M_BLOCKS], F32, name="bias")
         nc.sync.dma_start(windows[0][:], table[0:P, :])
-        nc.scalar.dma_start(weights_first[:], w_by_block[:, :, 0:P])
+        for kb in range(K_BLOCKS):
+            nc.scalar.dma_start(weights_first[kb][:], w[kb * P : (kb + 1) * P, 0:P])
         nc.sync.dma_start(offsets[:], offs)
         nc.sync.dma_start(windows[1][:], table[P : 2 * P, :])
         nc.scalar.dma_start(weights_rest[:], w_by_block[:, :, P:M])
@@ -37,7 +38,7 @@ def tile_gather_matmul_kernel(tc, table, w, b, offs, out):
 
         def weights(kb, mb):
             if mb == 0:
-                return weights_first[:, kb, :]
+                return weights_first[kb][:]
             return weights_rest[:, kb, (mb - 1) * P : mb * P]
 
         picked = [

@@ -25,7 +25,8 @@ def tile_gather_matmul_kernel(tc, table, w, b, offs, out):
         offsets = held.tile([P, N // 16], U16, name="offsets")
         windows = [held.tile([P, S], BF16, name=f"window{kb}") for kb in range(K_BLOCKS)]
         weights_first = [held.tile([P, P], BF16, name=f"weights_first{kb}") for kb in range(K_BLOCKS)]
-        weights_rest = held.tile([P, K_BLOCKS, M - P], BF16, name="weights_rest")
+        weights_second = held.tile([P, K_BLOCKS, P], BF16, name="weights_second")
+        weights_rest = held.tile([P, K_BLOCKS, M - 2 * P], BF16, name="weights_rest")
         w_by_block = w.rearrange("(kb p) m -> p kb m", p=P)
         bias = held.tile([P, M_BLOCKS], F32, name="bias")
         nc.sync.dma_start(windows[0][:], table[0:P, :])
@@ -33,13 +34,18 @@ def tile_gather_matmul_kernel(tc, table, w, b, offs, out):
             nc.scalar.dma_start(weights_first[kb][:], w[kb * P : (kb + 1) * P, 0:P])
         nc.sync.dma_start(offsets[:], offs)
         nc.sync.dma_start(windows[1][:], table[P : 2 * P, :])
-        nc.scalar.dma_start(weights_rest[:], w_by_block[:, :, P:M])
+        nc.vector.tensor_copy(weights_second[:, 0, 0:1], weights_first[0][:, 0:1])
+        nc.scalar.dma_start(weights_second[:], w_by_block[:, :, P : 2 * P])
+        nc.vector.tensor_copy(weights_rest[:, 0, 0:1], weights_first[0][:, 0:1])
+        nc.scalar.dma_start(weights_rest[:], w_by_block[:, :, 2 * P : M])
         nc.sync.dma_start(bias[:], b.rearrange("(mb p) o -> p (mb o)", p=P))
 
         def weights(kb, mb):
             if mb == 0:
                 return weights_first[kb][:]
-            return weights_rest[:, kb, (mb - 1) * P : mb * P]
+            if mb == 1:
+                return weights_second[:, kb, :]
+            return weights_rest[:, kb, (mb - 2) * P : (mb - 1) * P]
 
         picked = [
             offsets[:, piece * OFFSET_COLUMNS : (piece + 1) * OFFSET_COLUMNS] for piece in range(PIECES)

import concourse.mybir as mybir

BF16, F32, U16 = mybir.dt.bfloat16, mybir.dt.float32, mybir.dt.uint16
GELU = mybir.ActivationFunctionType.Gelu_apprx_tanh

P = 128
K, S = 256, 1024
M, N = 512, 1024
NEIGHBOURS = 16
PIECE = 512
K_BLOCKS, M_BLOCKS, PIECES = K // P, M // P, N // PIECE
OFFSET_COLUMNS = PIECE // 16
STEP = PIECE // 8

FLOPS = 2 * K * M * N


def tile_gather_matmul_kernel(tc, table, w, b, offs, out):
    nc = tc.nc
    with (
        tc.tile_pool(name="held", bufs=1) as held,
        tc.tile_pool(name="work", bufs=8) as work,
        tc.psum_pool(name="psum", bufs=4) as psum,
    ):
        offsets = held.tile([P, N // 16], U16, name="offsets")
        windows = [held.tile([P, S], BF16, name=f"window{kb}") for kb in range(K_BLOCKS)]
        weights_first = [held.tile([P, P], BF16, name=f"weights_first{kb}") for kb in range(K_BLOCKS)]
        weights_second = held.tile([P, K_BLOCKS, P], BF16, name="weights_second")
        weights_rest = held.tile([P, K_BLOCKS, M - 2 * P], BF16, name="weights_rest")
        w_by_block = w.rearrange("(kb p) m -> p kb m", p=P)
        bias = held.tile([P, M_BLOCKS], F32, name="bias")
        nc.sync.dma_start(windows[0][:], table[0:P, :])
        for kb in range(K_BLOCKS):
            nc.scalar.dma_start(weights_first[kb][:], w[kb * P : (kb + 1) * P, 0:P])
        nc.sync.dma_start(offsets[:], offs)
        nc.sync.dma_start(windows[1][:], table[P : 2 * P, :])
        nc.vector.tensor_copy(weights_second[:, 0, 0:1], weights_first[0][:, 0:1])
        nc.scalar.dma_start(weights_second[:], w_by_block[:, :, P : 2 * P])
        nc.vector.tensor_copy(weights_rest[:, 0, 0:1], weights_first[0][:, 0:1])
        nc.scalar.dma_start(weights_rest[:], w_by_block[:, :, 2 * P : M])
        nc.sync.dma_start(bias[:], b.rearrange("(mb p) o -> p (mb o)", p=P))

        def weights(kb, mb):
            if mb == 0:
                return weights_first[kb][:]
            if mb == 1:
                return weights_second[:, kb, :]
            return weights_rest[:, kb, (mb - 2) * P : (mb - 1) * P]

        picked = [
            offsets[:, piece * OFFSET_COLUMNS : (piece + 1) * OFFSET_COLUMNS] for piece in range(PIECES)
        ]
        for mb in range(M_BLOCKS):
            banks = [psum.tile([P, PIECE], F32, name=f"bank{piece}") for piece in range(PIECES)]
            if mb == 0:
                order = [(kb, piece) for kb in range(K_BLOCKS) for piece in range(PIECES)]
            else:
                order = [(kb, piece) for piece in range(PIECES) for kb in range(K_BLOCKS)]
            for kb, piece in order:
                nc.tensor.matmul(
                    banks[piece][:],
                    weights(kb, mb),
                    windows[kb][:].indirect(picked[piece]),
                    start=(kb == 0),
                    stop=(kb == K_BLOCKS - 1),
                )
            for piece in range(PIECES):
                pooled = work.tile([P, PIECE // NEIGHBOURS], F32, name="pooled")
                for step in range(PIECE // STEP):
                    z = work.tile([P, STEP], F32, name="z")
                    nc.scalar.activation(
                        z[:],
                        banks[piece][:, step * STEP : (step + 1) * STEP],
                        GELU,
                        bias=bias[:, mb : mb + 1],
                    )
                    first = step * STEP // NEIGHBOURS
                    nc.vector.tensor_reduce(
                        pooled[:, first : first + STEP // NEIGHBOURS],
                        z[:].rearrange("p (v t) -> p v t", t=NEIGHBOURS),
                        axis=mybir.AxisListType.X,
                        op=mybir.AluOpType.max,
                    )
                nodes = PIECE // NEIGHBOURS
                nc.sync.dma_start(out[mb * P : (mb + 1) * P, piece * nodes : (piece + 1) * nodes], pooled[:])
